import numpy as np
import ml_dtypes


def mxq(x, axis, fmt="e4m3"):
    dtype, down = {"e4m3": (ml_dtypes.float8_e4m3fn, 7), "e5m2": (ml_dtypes.float8_e5m2, 14)}[fmt]
    v = np.moveaxis(np.asarray(x, np.float32).astype(ml_dtypes.bfloat16).astype(np.float64), axis, -1)
    blocks = v.reshape(v.shape[:-1] + (-1, 32))
    amax = np.abs(blocks).max(-1, keepdims=True)
    byte = np.maximum(np.where(amax > 0, np.frexp(amax)[1] - 1 + 127, 0) - down, 1)
    scale = np.exp2(byte - 127.0)
    codes = (blocks / scale).astype(np.float32).astype(dtype).astype(np.float64)
    return np.moveaxis((codes * scale).reshape(v.shape), -1, axis)


WIDE = False


def mx_kscale(k):
    if not WIDE:
        return np.ones(k)
    levels = np.array([10, -10, 5, -5, 0])
    if k % 512:
        return np.exp2(np.random.permutation(np.resize(levels, k // 32))).repeat(32)
    a = np.empty((k // 512, 16))
    for p in range(k // 512):
        a[p, :8] = np.random.permutation(np.resize(levels, 8))
        for g in range(8):
            far = levels[np.abs(levels - a[p, g]) >= 10]
            a[p, g + 8] = far[np.random.randint(len(far))]
    return np.exp2(a.ravel()).repeat(32)


BF16 = ml_dtypes.bfloat16


def bf(x):
    return np.asarray(x, np.float32).astype(BF16)


def f64(x):
    return np.asarray(x).astype(np.float64)


E2M1 = np.array([0.0, 0.5, 1.0, 1.5, 2.0, 3.0, 4.0, 6.0, -0.0, -0.5, -1.0, -1.5, -2.0, -3.0, -4.0, -6.0])


def pack_weight(w, fmt):
    k, n = w.shape
    w = f64(bf(w)).reshape(k // 32, 32, n)
    amax = np.abs(w).max(1)
    if fmt == "e4m3":
        byte = np.frexp(amax)[1] - 1 + 127 - 7
    else:
        mant, ex = np.frexp(amax / 6.0)
        byte = np.where(mant > 0.5, ex, ex - 1) + 127
    byte = np.clip(np.where(amax > 0, byte, 1), 1, 254)
    scaled = (w * np.exp2(127.0 - byte)[:, None, :]).reshape(k, n).astype(np.float32)
    by_word = np.ascontiguousarray(scaled.reshape(k // 512, 128, 4, n).transpose(0, 1, 3, 2))
    if fmt == "e4m3":
        words = by_word.astype(ml_dtypes.float8_e4m3fn).view(np.uint8)
    else:
        c = by_word.astype(ml_dtypes.float4_e2m1fn).view(np.uint8) & 0xF
        words = c[..., 0::2] | (c[..., 1::2] << 4)
    return np.ascontiguousarray(words), np.ascontiguousarray(byte.astype(np.uint8).reshape(k // 512, 16, n))


def unpack_weight(words, scales, fmt):
    g, p, n, _ = words.shape
    if fmt == "e4m3":
        vals = np.ascontiguousarray(words).view(ml_dtypes.float8_e4m3fn).astype(np.float64)
    else:
        nib = np.empty((g, p, n, 4), np.uint8)
        nib[..., 0::2] = words & 0xF
        nib[..., 1::2] = words >> 4
        vals = E2M1[nib]
    vals = vals * np.repeat(np.exp2(scales.astype(np.float64) - 127.0), 8, axis=1)[..., None]
    return vals.transpose(0, 1, 3, 2).reshape(g * 512, n)
def pack4(w):
    words, scales = pack_weight(w, "e2m1")
    return words.reshape(words.shape[0], 128, -1), scales


def unpack4(words, scales):
    return unpack_weight(words.reshape(words.shape[0], 128, -1, 2), scales, "e2m1")


def planes(Y):
    n, m = Y.shape
    b = f64(bf(Y)).reshape(n // 32, 32, m)
    amax = np.abs(b).max(1)
    byte = np.clip(np.where(amax > 0, np.frexp(amax)[1] - 1 + 127 - 7, 1), 1, 254)
    codes = (b * np.exp2(127.0 - byte)[:, None, :]).reshape(n, m).astype(np.float32).astype(ml_dtypes.float8_e4m3fn).view(np.uint8)
    words = codes.reshape(n // 512, 128, 4, m).transpose(0, 1, 3, 2)
    return np.ascontiguousarray(words), np.ascontiguousarray(byte.astype(np.uint8).reshape(n // 512, 16, m))


G, R, T, C, D = 4, 512, 2048, 512, 512


def setup_inputs():
    s = mx_kscale(T)
    t = mx_kscale(C)
    rate = 0.3 * np.exp(0.5 * np.random.randn(T))
    idf = -np.log(-np.expm1(-rate))
    queries = np.log1p(np.random.poisson(rate, size=(G, R, T))) * idf
    term = np.random.randn(G, T, C) * np.sqrt(2.0 / T)
    doc = np.random.randn(G, C, D) / np.sqrt(C)
    term_words, term_scales = pack4((term / s[:, None]).reshape(G * T, C))
    doc_words, doc_scales = pack4((doc / t[:, None]).reshape(G * C, D))
    return {
        "queries": bf(queries * s),
        "term_words": term_words,
        "term_scales": term_scales,
        "concept_scale": bf(np.exp(0.5 * np.random.randn(G, C)) * t),
        "concept_shift": bf(0.4 * np.random.randn(G, C) * t),
        "doc_words": doc_words,
        "doc_scales": doc_scales,
        "doc_gain": bf(np.exp(0.8 * np.random.randn(G, D))),
        "doc_prior": bf(0.3 * np.random.randn(G, D)),
    }


def reference(queries, term_words, term_scales, concept_scale, concept_shift, doc_words, doc_scales, doc_gain, doc_prior):
    term = unpack4(term_words, term_scales).reshape(G, T, C)
    doc = unpack4(doc_words, doc_scales).reshape(G, C, D)
    h = mxq(f64(queries), 2, "e4m3") @ term
    z = h * f64(concept_scale)[:, None, :] + f64(concept_shift)[:, None, :]
    score = mxq(z, 2, "e4m3") @ doc
    y = score * f64(doc_gain)[:, None, :] + f64(doc_prior)[:, None, :]
    Y = y.reshape(G * R, D).T
    words, scales = planes(Y)
    return y, words, scales

@@ -1,0 +1,352 @@
+from contextlib import ExitStack
+
+import concourse.mybir as mybir
+from concourse.masks import make_identity
+
+G, R, T, C, D = 4, 512, 2048, 512, 512
+FLOPS = 2 * G * R * (T * C + C * D)
+
+F32 = mybir.dt.float32
+BF16 = mybir.dt.bfloat16
+I32 = mybir.dt.int32
+U32 = mybir.dt.uint32
+U8 = mybir.dt.uint8
+FP8X4 = mybir.dt.float8_e4m3fn_x4
+FP4X4 = mybir.dt.float4_e2m1fn_x4
+MULT = mybir.AluOpType.mult
+ADD = mybir.AluOpType.add
+
+P = 128
+PASSES = T // 512
+TILES_PER_COLLECTION = R // P
+TILES = G * TILES_PER_COLLECTION
+GP_TILES = 13
+V_SORT = 0
+S_SORT = 0
+Z_FIRST = TILES
+QSPLIT = 15
+VCAST = 15
+
+
+def tile_collection_concept_scores_k7_kernel(
+    tc, queries, term_words, term_scales, concept_scale, concept_shift,
+    doc_words, doc_scales, doc_gain, doc_prior, out_0, out_1, out_2,
+):
+    nc = tc.nc
+    query_rows = queries.rearrange("a r k -> (a r) k")
+    y_rows = out_0.rearrange("a r d -> (a r) d")
+    y_words = out_1[0].rearrange("p m t -> p (m t)").bitcast(I32)
+
+    with ExitStack() as ctx:
+        keep = ctx.enter_context(tc.tile_pool(name="keep", bufs=1))
+        work = ctx.enter_context(tc.tile_pool(name="work", bufs=3))
+        psum = ctx.enter_context(tc.psum_pool(name="psum", bufs=1))
+        ctx.enter_context(tc.manual_schedule())
+
+        identity = keep.tile([P, P], F32, name="identity")
+        make_identity(nc, identity[:])
+
+        q_raw = [[keep.tile([P, T // 2], BF16, name="q_raw%d_%d" % (i, half), align_bytes=64) for half in range(2)]
+                 if i == 0 else [keep.tile([P, T], BF16, name="q_raw%d" % i, align_bytes=64)] for i in range(TILES)]
+        term = [keep.tile([P, PASSES, 2 * C], U8, name="term%d" % a, align_bytes=64) for a in range(G)]
+        term_plane = [keep.tile([P, PASSES * C], U8, name="term_plane%d" % a, align_bytes=64) for a in range(G)]
+        doc = keep.tile([P, G, 2 * D], U8, name="doc", align_bytes=64)
+        doc_plane = keep.tile([P, G * D], U8, name="doc_plane", align_bytes=64)
+        scale = keep.tile([P, G * C], BF16, name="scale", align_bytes=64)
+        shift_words = keep.tile([P, G, 2], F32, name="shift_words", align_bytes=64)
+        gain = keep.tile([P, G * D], BF16, name="gain", align_bytes=64)
+        prior = keep.tile([P, G * D], BF16, name="prior", align_bytes=64)
+        y = [keep.tile([P, D], F32, name="y%d" % i, align_bytes=64) for i in range(TILES)]
+        y_codes = [keep.tile([P, R], U32, name="y_codes%d" % a, align_bytes=64) for a in range(G)]
+        y_plane = keep.tile([P, G * R], U8, name="y_plane", align_bytes=64)
+
+        for plane in term_plane + [doc_plane]:
+            nc.vector.memset(plane[:].bitcast(I32), 0)
+
+        def load_queries(i):
+            width = T // len(q_raw[i])
+            for n, piece in enumerate(q_raw[i]):
+                nc.sync.dma_start(out=piece[:], in_=query_rows[i * P:(i + 1) * P, n * width:(n + 1) * width])
+
+        def pass_words(i, first, count):
+            width = T // len(q_raw[i]) // 512
+            piece = q_raw[i][first // width]
+            return piece[:].bitcast(F32)[:, 256 * (first % width):256 * (first % width + count)]
+
+        def load_words(tile, words):
+            nc.sync.dma_start(out=tile[:].bitcast(I32), in_=words.rearrange("g p n -> p g n").bitcast(I32))
+
+        def load_plane(plane, scales):
+            groups = scales.shape[0]
+            for quadrant in range(4):
+                rows = plane[32 * quadrant:32 * quadrant + 4, :].rearrange("r (g n) -> r g n", g=groups)
+                nc.sync.dma_start(
+                    out=rows.bitcast(I32),
+                    in_=scales[:, 4 * quadrant:4 * quadrant + 4, :].rearrange("g r n -> r g n").bitcast(I32),
+                )
+
+        def load_term(a):
+            load_words(term[a], term_words[PASSES * a:PASSES * (a + 1)])
+            load_plane(term_plane[a], term_scales[PASSES * a:PASSES * (a + 1)])
+
+        def load_row(tile, vector, first, last):
+            nc.sync.dma_start(
+                out=tile[:, first * C:last * C],
+                in_=vector[first:last].rearrange("a n -> (a n)").partition_broadcast(P))
+
+        load_queries(0)
+        load_queries(1)
+        load_term(0)
+        load_queries(2)
+        nc.sync.dma_start(
+            out=shift_words[:], in_=concept_shift.rearrange("a (n m) -> n a m", m=4).bitcast(F32))
+        load_row(scale, concept_scale, 0, 1)
+        load_queries(3)
+        load_queries(4)
+        load_words(doc, doc_words)
+        load_plane(doc_plane, doc_scales)
+        load_term(1)
+        load_row(gain, doc_gain, 0, 1)
+        load_row(prior, doc_prior, 0, 1)
+        load_queries(5)
+        load_row(scale, concept_scale, 1, G)
+        load_queries(6)
+        load_queries(7)
+        load_term(2)
+        load_queries(8)
+        load_row(gain, doc_gain, 1, G)
+        load_queries(9)
+        load_row(prior, doc_prior, 1, G)
+        for i in range(10, TILES):
+            if i == 11:
+                load_term(3)
+            load_queries(i)
+
+        n_sorted = V_SORT + S_SORT
+        q_sorted, q_banks, q_bf, q_codes, q_plane, h, shift, z_bf, z_bank, z_grouped = (
+            {}, {}, {}, {}, {}, {}, {}, {}, {}, {})
+        z_codes, z_plane, score, y_scaled, y_bf, y_bank, y_grouped = {}, {}, {}, {}, {}, {}, {}
+
+        def sorted_pairs(ap):
+            return ap.rearrange("r (p u e) -> r u p e", u=2, e=2)
+
+        def cols(i):
+            a = i // TILES_PER_COLLECTION
+            return slice(a * C, (a + 1) * C)
+
+        def sort_words(copy, i, first, count):
+            if i not in q_sorted:
+                q_sorted[i] = work.tile([P, n_sorted, 2, P], F32, name="q_sorted", align_bytes=64)
+            at = first - (PASSES - n_sorted)
+            copy(out=q_sorted[i][:, at:at + count],
+                 in_=pass_words(i, first, count).rearrange("r (g p u) -> r g u p", u=2, g=count))
+
+        def turn_queries(i):
+            q_banks[i] = []
+            for half in range(2):
+                bank = psum.tile([P, 2, 2, P], F32, name="q_bank", tag="q_bank", bufs=3)
+                for g in range(2 * half, 2 * half + 2):
+                    for u in range(2):
+                        if i in q_sorted and g >= PASSES - n_sorted:
+                            words = q_sorted[i][:, g - (PASSES - n_sorted), u, :]
+                        else:
+                            words = pass_words(i, g, 1)[:, u::2]
+                        nc.tensor.transpose(bank[:, g % 2, u, :], words, identity[:])
+                q_banks[i].append(bank)
+
+        def group_queries(i):
+            q_bf[i] = [work.tile([P, 2 * P * 4], BF16, name="q_bf%d" % half, align_bytes=64) for half in range(2)] \
+                if i >= QSPLIT else [work.tile([P, PASSES * P * 4], BF16, name="q_bf", align_bytes=64)]
+            for half in range(2):
+                out = q_bf[i][half][:] if i >= QSPLIT else q_bf[i][0][:, half * 1024:(half + 1) * 1024]
+                nc.scalar.copy(
+                    out=out.bitcast(F32).rearrange("p (g r u) -> p g r u", u=2, g=2),
+                    in_=q_banks[i][half][:].rearrange("p g u r -> p g r u"))
+
+        def quantise_queries(i):
+            q_codes[i] = work.tile([P, PASSES * P], U32, name="q_codes", align_bytes=64)
+            q_plane[i] = work.tile([P, PASSES * P], U8, name="q_plane", align_bytes=64)
+            width = PASSES * P // len(q_bf[i])
+            for n, piece in enumerate(q_bf[i]):
+                part = slice(n * width, (n + 1) * width)
+                nc.vector.quantize_mx(out=q_codes[i][:, part].bitcast(FP8X4), scales=q_plane[i][:, part], in_=piece[:])
+
+        def first_product(i):
+            a = i // TILES_PER_COLLECTION
+            h[i] = (psum.tile([P, C], F32, name="h", tag="h") if i < TILES - 1
+                    else psum.tile([P, C], F32, name="last_h", tag="q_bank", bufs=3))
+            for g in range(PASSES):
+                nc.tensor.matmul_mx(
+                    out=h[i][:],
+                    lhsT=q_codes[i][:, g * P:(g + 1) * P].bitcast(FP8X4),
+                    lhsT_scale=q_plane[i][:, g * P:(g + 1) * P],
+                    rhs=term[a][:, g, :].bitcast(FP4X4),
+                    rhs_scale=term_plane[a][:, g * C:(g + 1) * C],
+                    start=(g == 0), stop=(g == PASSES - 1))
+
+        def spread_shift(a):
+            shift[a] = psum.tile([P, 2, P], F32, name="shift")
+            for u in range(2):
+                nc.tensor.transpose(shift[a][:, u, :], shift_words[:, a, u:u + 1].to_broadcast([P, P]), identity[:])
+
+        def make_z(i):
+            a = i // TILES_PER_COLLECTION
+            z_scaled = [work.tile([P, C // 2], F32, name="z_scaled%d" % u) for u in range(2)]
+            for u in range(2):
+                nc.vector.tensor_tensor(
+                    out=z_scaled[u][:].rearrange("r (p e) -> r p e", e=2),
+                    in0=sorted_pairs(h[i][:])[:, u], in1=sorted_pairs(scale[:, cols(i)])[:, u], op=MULT)
+            z_bf[i] = work.tile([P, C], BF16, name="z_bf", align_bytes=64)
+            for u in range(2):
+                nc.vector.tensor_tensor(
+                    out=z_bf[i][:, u * 256:(u + 1) * 256], in0=z_scaled[u][:],
+                    in1=shift[a][:, u, :].bitcast(BF16), op=ADD)
+
+        def turn(source, name):
+            bank = psum.tile([P, 2, P], F32, name="bank", tag=name)
+            words = source[:].bitcast(F32)
+            for u in range(2):
+                nc.tensor.transpose(bank[:, u, :], words[:, u * P:(u + 1) * P], identity[:])
+            return bank
+
+        def group(bank, name):
+            grouped = work.tile([P, P * 4], BF16, name=name, align_bytes=64)
+            nc.scalar.copy(
+                out=grouped[:].bitcast(F32).rearrange("p (r u) -> p r u", u=2),
+                in_=bank[:].rearrange("p u r -> p r u"))
+            return grouped
+
+        def quantise_z(i):
+            z_codes[i] = work.tile([P, P], U32, name="z_codes", align_bytes=64)
+            z_plane[i] = work.tile([P, P], U8, name="z_plane", align_bytes=64)
+            nc.vector.quantize_mx(out=z_codes[i][:].bitcast(FP8X4), scales=z_plane[i][:], in_=z_grouped[i][:])
+
+        def second_product(i):
+            a = i // TILES_PER_COLLECTION
+            score[i] = (psum.tile([P, D], F32, name="score") if i < TILES - 3
+                        else psum.tile([P, D], F32, name="late_score", tag="q_bank", bufs=3))
+            nc.tensor.matmul_mx(
+                out=score[i][:],
+                lhsT=z_codes[i][:].bitcast(FP8X4), lhsT_scale=z_plane[i][:],
+                rhs=doc[:, a, :].bitcast(FP4X4), rhs_scale=doc_plane[:, a * D:(a + 1) * D],
+                start=True, stop=True)
+
+        def scale_y(i):
+            y_scaled[i] = work.tile([P, D], F32, name="y_scaled", bufs=4)
+            nc.vector.tensor_tensor(out=y_scaled[i][:], in0=score[i][:], in1=gain[:, cols(i)], op=MULT)
+            if i < GP_TILES:
+                nc.gpsimd.tensor_tensor(out=y[i][:], in0=y_scaled[i][:], in1=prior[:, cols(i)], op=ADD)
+
+        def shift_y(i):
+            if i >= VCAST:
+                y_bf[i] = work.tile([P, D], BF16, name="y_bf", align_bytes=64)
+                nc.vector.tensor_tensor(
+                    out=y_bf[i][:].rearrange("r (u p e) -> r u p e", u=2, e=2),
+                    in0=sorted_pairs(y_scaled[i][:]), in1=sorted_pairs(prior[:, cols(i)]), op=ADD)
+            if i >= GP_TILES:
+                nc.vector.tensor_tensor(out=y[i][:], in0=y_scaled[i][:], in1=prior[:, cols(i)], op=ADD)
+
+        def round_y(i):
+            if i < VCAST:
+                y_bf[i] = work.tile([P, D], BF16, name="y_bf", align_bytes=64)
+                nc.scalar.copy(out=y_bf[i][:].rearrange("r (u p e) -> r u p e", u=2, e=2), in_=sorted_pairs(y[i][:]))
+            nc.sync.dma_start(out=y_rows[i * P:(i + 1) * P, :], in_=y[i][:])
+
+        def quantise_y(i):
+            a, j = divmod(i, TILES_PER_COLLECTION)
+            nc.vector.quantize_mx(
+                out=y_codes[a][:, j * P:(j + 1) * P].bitcast(FP8X4),
+                scales=y_plane[:, i * P:(i + 1) * P], in_=y_grouped[i][:])
+
+        def store_codes(i):
+            a, j = divmod(i, TILES_PER_COLLECTION)
+            if j == TILES_PER_COLLECTION - 1:
+                nc.sync.dma_start(out=y_words[:, a * R:(a + 1) * R], in_=y_codes[a][:].bitcast(I32))
+
+        def turn_z(i):
+            z_grouped[i] = group(turn(z_bf[i], "z_bank"), "z_grouped")
+
+        def turn_y(i):
+            y_grouped[i] = group(turn(y_bf[i], {TILES - 2: "h", TILES - 1: "z_bank"}.get(i, "y_bank")), "y_grouped")
+
+        def store_plane(first, last):
+            for quadrant in range(4):
+                nc.sync.dma_start(
+                    out=out_2[0, 4 * quadrant:4 * quadrant + 4, first * P:last * P].bitcast(I32),
+                    in_=y_plane[32 * quadrant:32 * quadrant + 4, first * P:last * P].bitcast(I32))
+
+        for step in range(TILES):
+            if step % TILES_PER_COLLECTION == 2:
+                spread_shift(step // TILES_PER_COLLECTION)
+            if step >= 3:
+                turn_z(step - 3)
+            if step >= 6:
+                turn_y(step - 6)
+            turn_queries(step)
+            group_queries(step)
+            if step >= 5:
+                scale_y(step - 5)
+            if step >= 2:
+                make_z(step - 2)
+            if step >= 3:
+                quantise_z(step - 3)
+            if step >= 6:
+                quantise_y(step - 6)
+            if step >= 5:
+                shift_y(step - 5)
+            if V_SORT and step + 1 < TILES:
+                sort_words(nc.vector.tensor_copy, step + 1, PASSES - n_sorted, V_SORT)
+            quantise_queries(step)
+            if step >= 5:
+                round_y(step - 5)
+            if S_SORT and step + 1 < TILES:
+                sort_words(nc.scalar.copy, step + 1, PASSES - S_SORT, S_SORT)
+            if step >= 6:
+                store_codes(step - 6)
+            if step >= 4:
+                second_product(step - 4)
+            if step >= 1:
+                first_product(step - 1)
+
+        first_product(15)
+        turn_z(13)
+        turn_y(10)
+        scale_y(11)
+        make_z(14)
+        second_product(12)
+        make_z(15)
+        turn_z(14)
+        round_y(11)
+        quantise_z(13)
+        turn_z(15)
+        quantise_z(14)
+        quantise_y(10)
+        second_product(13)
+        second_product(14)
+        turn_y(11)
+        scale_y(12)
+        quantise_z(15)
+        second_product(15)
+        scale_y(13)
+        scale_y(14)
+        scale_y(15)
+        quantise_y(11)
+        store_codes(11)
+        store_plane(0, 12)
+        round_y(12)
+        shift_y(13)
+        round_y(13)
+        turn_y(12)
+        shift_y(14)
+        round_y(14)
+        turn_y(13)
+        shift_y(15)
+        turn_y(14)
+        turn_y(15)
+        round_y(15)
+        quantise_y(12)
+        quantise_y(13)
+        quantise_y(14)
+        quantise_y(15)
+        store_codes(15)
+        store_plane(12, 16)

@@ -20,7 +20,7 @@ P = 128
 PASSES = T // 512
 TILES_PER_COLLECTION = R // P
 TILES = G * TILES_PER_COLLECTION
-GP_TILES = 13
+GP_TILES = TILES - 2
 V_SORT = 0
 S_SORT = 0
 Z_FIRST = TILES
@@ -52,10 +52,8 @@ def tile_collection_concept_scores_k7_kernel(
         term_plane = [keep.tile([P, PASSES * C], U8, name="term_plane%d" % a, align_bytes=64) for a in range(G)]
         doc = keep.tile([P, G, 2 * D], U8, name="doc", align_bytes=64)
         doc_plane = keep.tile([P, G * D], U8, name="doc_plane", align_bytes=64)
-        scale = keep.tile([P, G * C], BF16, name="scale", align_bytes=64)
-        shift_words = keep.tile([P, G, 2], F32, name="shift_words", align_bytes=64)
-        gain = keep.tile([P, G * D], BF16, name="gain", align_bytes=64)
-        prior = keep.tile([P, G * D], BF16, name="prior", align_bytes=64)
+        row_words = [keep.tile([P, G, 2], F32, name="row_words%d" % n, align_bytes=64) for n in range(4)]
+        terms = psum.tile([P, 2, 2, P], F32, name="terms")
         y = [keep.tile([P, D], F32, name="y%d" % i, align_bytes=64) for i in range(TILES)]
         y_codes = [keep.tile([P, R], U32, name="y_codes%d" % a, align_bytes=64) for a in range(G)]
         y_plane = keep.tile([P, G * R], U8, name="y_plane", align_bytes=64)
@@ -89,50 +87,35 @@ def tile_collection_concept_scores_k7_kernel(
             load_words(term[a], term_words[PASSES * a:PASSES * (a + 1)])
             load_plane(term_plane[a], term_scales[PASSES * a:PASSES * (a + 1)])
 
-        def load_row(tile, vector, first, last):
-            nc.sync.dma_start(
-                out=tile[:, first * C:last * C],
-                in_=vector[first:last].rearrange("a n -> (a n)").partition_broadcast(P))
+        def load_row(tile, vector):
+            nc.sync.dma_start(out=tile[:], in_=vector.rearrange("a (n m) -> n a m", m=4).bitcast(F32))
 
         load_queries(0)
+        load_row(row_words[0], concept_scale)
         load_queries(1)
         load_term(0)
         load_queries(2)
-        nc.sync.dma_start(
-            out=shift_words[:], in_=concept_shift.rearrange("a (n m) -> n a m", m=4).bitcast(F32))
-        load_row(scale, concept_scale, 0, 1)
+        load_row(row_words[1], concept_shift)
+        load_row(row_words[2], doc_gain)
         load_queries(3)
-        load_queries(4)
         load_words(doc, doc_words)
         load_plane(doc_plane, doc_scales)
-        load_term(1)
-        load_row(gain, doc_gain, 0, 1)
-        load_row(prior, doc_prior, 0, 1)
-        load_queries(5)
-        load_row(scale, concept_scale, 1, G)
-        load_queries(6)
-        load_queries(7)
-        load_term(2)
-        load_queries(8)
-        load_row(gain, doc_gain, 1, G)
-        load_queries(9)
-        load_row(prior, doc_prior, 1, G)
-        for i in range(10, TILES):
-            if i == 11:
-                load_term(3)
+        load_row(row_words[3], doc_prior)
+        load_queries(4)
+        for i in range(5, TILES):
+            if i % TILES_PER_COLLECTION == 1 and i < TILES - 1:
+                load_term(i // TILES_PER_COLLECTION)
             load_queries(i)
 
         n_sorted = V_SORT + S_SORT
-        q_sorted, q_banks, q_bf, q_codes, q_plane, h, shift, z_bf, z_bank, z_grouped = (
+        q_sorted, q_banks, q_bf, q_codes, q_plane, h, z_scaled, z_bf, z_bank, z_grouped = (
             {}, {}, {}, {}, {}, {}, {}, {}, {}, {})
         z_codes, z_plane, score, y_scaled, y_bf, y_bank, y_grouped = {}, {}, {}, {}, {}, {}, {}
 
         def sorted_pairs(ap):
             return ap.rearrange("r (p u e) -> r u p e", u=2, e=2)
 
-        def cols(i):
-            a = i // TILES_PER_COLLECTION
-            return slice(a * C, (a + 1) * C)
+        factor = {}
 
         def sort_words(copy, i, first, count):
             if i not in q_sorted:
@@ -184,23 +167,34 @@ def tile_collection_concept_scores_k7_kernel(
                     rhs_scale=term_plane[a][:, g * C:(g + 1) * C],
                     start=(g == 0), stop=(g == PASSES - 1))
 
-        def spread_shift(a):
-            shift[a] = psum.tile([P, 2, P], F32, name="shift")
+        def spread(words, a, out):
             for u in range(2):
-                nc.tensor.transpose(shift[a][:, u, :], shift_words[:, a, u:u + 1].to_broadcast([P, P]), identity[:])
+                nc.tensor.transpose(out[:, u, :], words[:, a, u:u + 1].to_broadcast([P, P]), identity[:])
 
-        def make_z(i):
-            a = i // TILES_PER_COLLECTION
-            z_scaled = [work.tile([P, C // 2], F32, name="z_scaled%d" % u) for u in range(2)]
-            for u in range(2):
-                nc.vector.tensor_tensor(
-                    out=z_scaled[u][:].rearrange("r (p e) -> r p e", e=2),
-                    in0=sorted_pairs(h[i][:])[:, u], in1=sorted_pairs(scale[:, cols(i)])[:, u], op=MULT)
+        def spread_term(a, n):
+            spread(row_words[2 * n + 1], a, terms[:, n])
+
+        def spread_factor(a, n):
+            bank = psum.tile([P, 2, P], F32, name="bank", tag="y_bank")
+            spread(row_words[2 * n], a, bank)
+            row = work.tile([P, 2 * P], F32, name="factor%d" % n, bufs=2)
+            if n == 0:
+                nc.scalar.copy(out=row[:], in_=bank[:].rearrange("r u p -> r (u p)"))
+            else:
+                nc.scalar.copy(out=row[:].rearrange("r (p u) -> r p u", u=2), in_=bank[:].rearrange("r u p -> r p u"))
+            factor[n, a] = row
+
+        def scale_z(i):
+            z_scaled[i] = work.tile([P, C], F32, name="z_scaled")
+            nc.vector.tensor_tensor(
+                out=z_scaled[i][:].rearrange("r (u p e) -> r u p e", u=2, e=2), in0=sorted_pairs(h[i][:]),
+                in1=factor[0, i // TILES_PER_COLLECTION][:].bitcast(BF16).rearrange("r (u p e) -> r u p e", u=2, e=2), op=MULT)
+
+        def shift_z(i):
             z_bf[i] = work.tile([P, C], BF16, name="z_bf", align_bytes=64)
-            for u in range(2):
-                nc.vector.tensor_tensor(
-                    out=z_bf[i][:, u * 256:(u + 1) * 256], in0=z_scaled[u][:],
-                    in1=shift[a][:, u, :].bitcast(BF16), op=ADD)
+            nc.vector.tensor_tensor(
+                out=z_bf[i][:], in0=z_scaled[i][:],
+                in1=terms[:, 0].rearrange("r u p -> r (u p)").bitcast(BF16), op=ADD)
 
         def turn(source, name):
             bank = psum.tile([P, 2, P], F32, name="bank", tag=name)
@@ -223,7 +217,7 @@ def tile_collection_concept_scores_k7_kernel(
 
         def second_product(i):
             a = i // TILES_PER_COLLECTION
-            score[i] = (psum.tile([P, D], F32, name="score") if i < TILES - 3
+            score[i] = (psum.tile([P, D], F32, name="score") if i < TILES - 2
                         else psum.tile([P, D], F32, name="late_score", tag="q_bank", bufs=3))
             nc.tensor.matmul_mx(
                 out=score[i][:],
@@ -233,18 +227,19 @@ def tile_collection_concept_scores_k7_kernel(
 
         def scale_y(i):
             y_scaled[i] = work.tile([P, D], F32, name="y_scaled", bufs=4)
-            nc.vector.tensor_tensor(out=y_scaled[i][:], in0=score[i][:], in1=gain[:, cols(i)], op=MULT)
-            if i < GP_TILES:
-                nc.gpsimd.tensor_tensor(out=y[i][:], in0=y_scaled[i][:], in1=prior[:, cols(i)], op=ADD)
+            nc.vector.tensor_tensor(out=y_scaled[i][:], in0=score[i][:], in1=factor[1, i // TILES_PER_COLLECTION][:].bitcast(BF16), op=MULT)
 
         def shift_y(i):
+            prior = terms[:, 1].bitcast(BF16).rearrange("r u (p e) -> r u p e", e=2)
             if i >= VCAST:
                 y_bf[i] = work.tile([P, D], BF16, name="y_bf", align_bytes=64)
                 nc.vector.tensor_tensor(
                     out=y_bf[i][:].rearrange("r (u p e) -> r u p e", u=2, e=2),
-                    in0=sorted_pairs(y_scaled[i][:]), in1=sorted_pairs(prior[:, cols(i)]), op=ADD)
-            if i >= GP_TILES:
-                nc.vector.tensor_tensor(out=y[i][:], in0=y_scaled[i][:], in1=prior[:, cols(i)], op=ADD)
+                    in0=sorted_pairs(y_scaled[i][:]), in1=prior, op=ADD)
+            nc.vector.tensor_tensor(
+                out=y[i][:].rearrange("r (p u e) -> r p u e", u=2, e=2),
+                in0=y_scaled[i][:].rearrange("r (p u e) -> r p u e", u=2, e=2),
+                in1=prior.rearrange("r u p e -> r p u e"), op=ADD)
 
         def round_y(i):
             if i < VCAST:
@@ -276,75 +271,79 @@ def tile_collection_concept_scores_k7_kernel(
                     in_=y_plane[32 * quadrant:32 * quadrant + 4, first * P:last * P].bitcast(I32))
 
         for step in range(TILES):
-            if step % TILES_PER_COLLECTION == 2:
-                spread_shift(step // TILES_PER_COLLECTION)
             if step >= 3:
                 turn_z(step - 3)
-            if step >= 6:
-                turn_y(step - 6)
+            if step % TILES_PER_COLLECTION == 2:
+                spread_term(step // TILES_PER_COLLECTION, 0)
+            if step % TILES_PER_COLLECTION == 0 and step >= 4:
+                spread_term(step // TILES_PER_COLLECTION - 1, 1)
+            if step % 2 == 1:
+                spread_factor(step // TILES_PER_COLLECTION, step % TILES_PER_COLLECTION // 2)
+            if S_SORT and step + 1 < TILES:
+                sort_words(nc.scalar.copy, step + 1, PASSES - S_SORT, S_SORT)
             turn_queries(step)
             group_queries(step)
             if step >= 5:
-                scale_y(step - 5)
+                turn_y(step - 5)
             if step >= 2:
-                make_z(step - 2)
+                scale_z(step - 2)
+            if step >= 4:
+                scale_y(step - 4)
+            if step >= 2:
+                shift_z(step - 2)
             if step >= 3:
                 quantise_z(step - 3)
-            if step >= 6:
-                quantise_y(step - 6)
-            if step >= 5:
-                shift_y(step - 5)
+            if step >= 4:
+                shift_y(step - 4)
             if V_SORT and step + 1 < TILES:
                 sort_words(nc.vector.tensor_copy, step + 1, PASSES - n_sorted, V_SORT)
             quantise_queries(step)
             if step >= 5:
-                round_y(step - 5)
-            if S_SORT and step + 1 < TILES:
-                sort_words(nc.scalar.copy, step + 1, PASSES - S_SORT, S_SORT)
-            if step >= 6:
-                store_codes(step - 6)
+                quantise_y(step - 5)
+                store_codes(step - 5)
             if step >= 4:
-                second_product(step - 4)
+                round_y(step - 4)
             if step >= 1:
                 first_product(step - 1)
+            if step >= 3:
+                second_product(step - 3)
 
-        first_product(15)
+        spread_term(G - 1, 1)
         turn_z(13)
-        turn_y(10)
-        scale_y(11)
-        make_z(14)
-        second_product(12)
-        make_z(15)
-        turn_z(14)
-        round_y(11)
-        quantise_z(13)
-        turn_z(15)
-        quantise_z(14)
-        quantise_y(10)
-        second_product(13)
-        second_product(14)
+        first_product(15)
         turn_y(11)
+        scale_z(14)
         scale_y(12)
-        quantise_z(15)
-        second_product(15)
-        scale_y(13)
-        scale_y(14)
-        scale_y(15)
+        shift_z(14)
+        quantise_z(13)
+        scale_z(15)
+        shift_y(12)
+        shift_z(15)
+        turn_z(14)
+        second_product(13)
+        round_y(12)
         quantise_y(11)
         store_codes(11)
         store_plane(0, 12)
-        round_y(12)
-        shift_y(13)
-        round_y(13)
+        turn_z(15)
+        quantise_z(14)
+        scale_y(13)
+        second_product(14)
         turn_y(12)
+        quantise_z(15)
+        second_product(15)
+        shift_y(13)
+        scale_y(14)
+        round_y(13)
+        scale_y(15)
         shift_y(14)
-        round_y(14)
+        quantise_y(12)
         turn_y(13)
+        round_y(14)
         shift_y(15)
         turn_y(14)
         turn_y(15)
         round_y(15)
-        quantise_y(12)
         quantise_y(13)
         quantise_y(14)
         quantise_y(15)

@@ -20,9 +20,16 @@ P = 128
 PASSES = T // 512
 TILES_PER_COLLECTION = R // P
 TILES = G * TILES_PER_COLLECTION
-GP_TILES = TILES - 2
+GP_TILES = 12
 V_SORT = 0
-S_SORT = 0
+G_SORT = 0
+S_SORT = 1
+SORT_FROM = 2
+EARLY = 1
+YLATE = 0
+QFIRST = 0
+GCOLS = 256
+LAG = 0
 Z_FIRST = TILES
 QSPLIT = 15
 VCAST = 15
@@ -52,12 +59,14 @@ def tile_collection_concept_scores_k7_kernel(
         term_plane = [keep.tile([P, PASSES * C], U8, name="term_plane%d" % a, align_bytes=64) for a in range(G)]
         doc = keep.tile([P, G, 2 * D], U8, name="doc", align_bytes=64)
         doc_plane = keep.tile([P, G * D], U8, name="doc_plane", align_bytes=64)
-        row_words = [keep.tile([P, G, 2], F32, name="row_words%d" % n, align_bytes=64) for n in range(4)]
-        terms = psum.tile([P, 2, 2, P], F32, name="terms")
+        row_raw = keep.tile([P, P], F32, name="row_raw", align_bytes=64)
+        row_words = keep.tile([P, 8 * G], F32, name="row_words", align_bytes=64)
+        terms = psum.tile([P, 2, 2 * P], F32, name="terms")
         y = [keep.tile([P, D], F32, name="y%d" % i, align_bytes=64) for i in range(TILES)]
         y_codes = [keep.tile([P, R], U32, name="y_codes%d" % a, align_bytes=64) for a in range(G)]
         y_plane = keep.tile([P, G * R], U8, name="y_plane", align_bytes=64)
 
+        nc.vector.memset(row_raw[:], 0.0)
         for plane in term_plane + [doc_plane]:
             nc.vector.memset(plane[:].bitcast(I32), 0)
 
@@ -87,27 +96,27 @@ def tile_collection_concept_scores_k7_kernel(
             load_words(term[a], term_words[PASSES * a:PASSES * (a + 1)])
             load_plane(term_plane[a], term_scales[PASSES * a:PASSES * (a + 1)])
 
-        def load_row(tile, vector):
-            nc.sync.dma_start(out=tile[:], in_=vector.rearrange("a (n m) -> n a m", m=4).bitcast(F32))
+        def load_row(n, vector):
+            nc.sync.dma_start(
+                out=row_raw[2 * G * n:2 * G * (n + 1), :],
+                in_=vector.rearrange("a (j m) -> (a j) m", j=2).bitcast(F32))
 
         load_queries(0)
-        load_row(row_words[0], concept_scale)
+        for n, vector in enumerate((concept_scale, concept_shift, doc_gain, doc_prior)):
+            load_row(n, vector)
         load_queries(1)
         load_term(0)
         load_queries(2)
-        load_row(row_words[1], concept_shift)
-        load_row(row_words[2], doc_gain)
         load_queries(3)
         load_words(doc, doc_words)
         load_plane(doc_plane, doc_scales)
-        load_row(row_words[3], doc_prior)
         load_queries(4)
         for i in range(5, TILES):
             if i % TILES_PER_COLLECTION == 1 and i < TILES - 1:
                 load_term(i // TILES_PER_COLLECTION)
             load_queries(i)
 
-        n_sorted = V_SORT + S_SORT
+        n_sorted = V_SORT + S_SORT + G_SORT
         q_sorted, q_banks, q_bf, q_codes, q_plane, h, z_scaled, z_bf, z_bank, z_grouped = (
             {}, {}, {}, {}, {}, {}, {}, {}, {}, {})
         z_codes, z_plane, score, y_scaled, y_bf, y_bank, y_grouped = {}, {}, {}, {}, {}, {}, {}
@@ -115,18 +124,19 @@ def tile_collection_concept_scores_k7_kernel(
         def sorted_pairs(ap):
             return ap.rearrange("r (p u e) -> r u p e", u=2, e=2)
 
-        factor = {}
+        rows = {}
 
         def sort_words(copy, i, first, count):
             if i not in q_sorted:
-                q_sorted[i] = work.tile([P, n_sorted, 2, P], F32, name="q_sorted", align_bytes=64)
+                q_sorted[i] = work.tile([P, n_sorted, 2, P], F32, name="q_sorted", align_bytes=64, bufs=1 if G_SORT else 3)
             at = first - (PASSES - n_sorted)
             copy(out=q_sorted[i][:, at:at + count],
                  in_=pass_words(i, first, count).rearrange("r (g p u) -> r g u p", u=2, g=count))
 
         def turn_queries(i):
             q_banks[i] = []
-            for half in range(2):
+            q_banks[i] = [None, None]
+            for half in ((1, 0) if G_SORT else (0, 1)):
                 bank = psum.tile([P, 2, 2, P], F32, name="q_bank", tag="q_bank", bufs=3)
                 for g in range(2 * half, 2 * half + 2):
                     for u in range(2):
@@ -135,12 +145,12 @@ def tile_collection_concept_scores_k7_kernel(
                         else:
                             words = pass_words(i, g, 1)[:, u::2]
                         nc.tensor.transpose(bank[:, g % 2, u, :], words, identity[:])
-                q_banks[i].append(bank)
+                q_banks[i][half] = bank
 
         def group_queries(i):
             q_bf[i] = [work.tile([P, 2 * P * 4], BF16, name="q_bf%d" % half, align_bytes=64) for half in range(2)] \
                 if i >= QSPLIT else [work.tile([P, PASSES * P * 4], BF16, name="q_bf", align_bytes=64)]
-            for half in range(2):
+            for half in ((1, 0) if G_SORT else (0, 1)):
                 out = q_bf[i][half][:] if i >= QSPLIT else q_bf[i][0][:, half * 1024:(half + 1) * 1024]
                 nc.scalar.copy(
                     out=out.bitcast(F32).rearrange("p (g r u) -> p g r u", u=2, g=2),
@@ -167,37 +177,50 @@ def tile_collection_concept_scores_k7_kernel(
                     rhs_scale=term_plane[a][:, g * C:(g + 1) * C],
                     start=(g == 0), stop=(g == PASSES - 1))
 
-        def spread(words, a, out):
-            for u in range(2):
-                nc.tensor.transpose(out[:, u, :], words[:, a, u:u + 1].to_broadcast([P, P]), identity[:])
+        def turn_rows():
+            bank = psum.tile([P, P], F32, name="bank", tag="y_bank")
+            nc.tensor.transpose(bank[:], row_raw[:], identity[:])
+            nc.scalar.copy(out=row_words[:], in_=bank[:, :8 * G])
 
-        def spread_term(a, n):
-            spread(row_words[2 * n + 1], a, terms[:, n])
+        def spread(n, a, j, out):
+            column = 2 * G * n + 2 * a + j
+            nc.tensor.transpose(
+                out[:, j * P:(j + 1) * P], row_words[:, column:column + 1].to_broadcast([P, P]), identity[:])
 
-        def spread_factor(a, n):
-            bank = psum.tile([P, 2, P], F32, name="bank", tag="y_bank")
-            spread(row_words[2 * n], a, bank)
-            row = work.tile([P, 2 * P], F32, name="factor%d" % n, bufs=2)
+        def spread_row(a, n, staging):
+            shared = n == 3 and a * TILES_PER_COLLECTION < GP_TILES
+            for j in range(2):
+                spread(n, a, j, staging if n % 2 == 0 or (shared and j == 0) else terms[:, n // 2])
+
+        def keep_row(a, n, staging):
             if n == 0:
-                nc.scalar.copy(out=row[:], in_=bank[:].rearrange("r u p -> r (u p)"))
-            else:
-                nc.scalar.copy(out=row[:].rearrange("r (p u) -> r p u", u=2), in_=bank[:].rearrange("r u p -> r p u"))
-            factor[n, a] = row
+                rows[n, a] = work.tile([P, 2 * P], F32, name="scale", bufs=2)
+                nc.scalar.copy(out=rows[n, a][:].rearrange("r (u p) -> r u p", u=2),
+                               in_=staging.rearrange("r (p u) -> r u p", u=2))
+            elif n == 2:
+                rows[n, a] = work.tile([P, 2 * P], F32, name="gain", bufs=2)
+                nc.scalar.copy(out=rows[n, a][:], in_=staging)
+            elif n == 3 and a * TILES_PER_COLLECTION < GP_TILES:
+                rows[n, a] = work.tile([P, P], F32, name="prior", bufs=2)
+                nc.scalar.copy(out=rows[n, a][:], in_=staging[:, :P])
 
         def scale_z(i):
             z_scaled[i] = work.tile([P, C], F32, name="z_scaled")
             nc.vector.tensor_tensor(
                 out=z_scaled[i][:].rearrange("r (u p e) -> r u p e", u=2, e=2), in0=sorted_pairs(h[i][:]),
-                in1=factor[0, i // TILES_PER_COLLECTION][:].bitcast(BF16).rearrange("r (u p e) -> r u p e", u=2, e=2), op=MULT)
+                in1=rows[0, i // TILES_PER_COLLECTION][:].bitcast(BF16).rearrange("r (u p e) -> r u p e", u=2, e=2),
+                op=MULT)
 
         def shift_z(i):
             z_bf[i] = work.tile([P, C], BF16, name="z_bf", align_bytes=64)
             nc.vector.tensor_tensor(
-                out=z_bf[i][:], in0=z_scaled[i][:],
-                in1=terms[:, 0].rearrange("r u p -> r (u p)").bitcast(BF16), op=ADD)
+                out=z_bf[i][:].rearrange("r (u p e) -> r u p e", u=2, e=2),
+                in0=z_scaled[i][:].rearrange("r (u p e) -> r u p e", u=2, e=2),
+                in1=sorted_pairs(terms[:, 0].bitcast(BF16)), op=ADD)
 
-        def turn(source, name):
-            bank = psum.tile([P, 2, P], F32, name="bank", tag=name)
+        def turn(source, name, bank=None):
+            if bank is None:
+                bank = psum.tile([P, 2, P], F32, name="bank", tag=name)
             words = source[:].bitcast(F32)
             for u in range(2):
                 nc.tensor.transpose(bank[:, u, :], words[:, u * P:(u + 1) * P], identity[:])
@@ -227,19 +250,21 @@ def tile_collection_concept_scores_k7_kernel(
 
         def scale_y(i):
             y_scaled[i] = work.tile([P, D], F32, name="y_scaled", bufs=4)
-            nc.vector.tensor_tensor(out=y_scaled[i][:], in0=score[i][:], in1=factor[1, i // TILES_PER_COLLECTION][:].bitcast(BF16), op=MULT)
+            nc.vector.tensor_tensor(out=y_scaled[i][:], in0=score[i][:], in1=rows[2, i // TILES_PER_COLLECTION][:].bitcast(BF16), op=MULT)
+            if i < GP_TILES:
+                nc.gpsimd.tensor_tensor(
+                    out=y[i][:, :GCOLS], in0=y_scaled[i][:, :GCOLS], in1=rows[3, i // TILES_PER_COLLECTION][:].bitcast(BF16), op=ADD)
 
         def shift_y(i):
-            prior = terms[:, 1].bitcast(BF16).rearrange("r u (p e) -> r u p e", e=2)
+            prior = terms[:, 1].bitcast(BF16)
             if i >= VCAST:
                 y_bf[i] = work.tile([P, D], BF16, name="y_bf", align_bytes=64)
                 nc.vector.tensor_tensor(
                     out=y_bf[i][:].rearrange("r (u p e) -> r u p e", u=2, e=2),
-                    in0=sorted_pairs(y_scaled[i][:]), in1=prior, op=ADD)
-            nc.vector.tensor_tensor(
-                out=y[i][:].rearrange("r (p u e) -> r p u e", u=2, e=2),
-                in0=y_scaled[i][:].rearrange("r (p u e) -> r p u e", u=2, e=2),
-                in1=prior.rearrange("r u p e -> r p u e"), op=ADD)
+                    in0=sorted_pairs(y_scaled[i][:]), in1=sorted_pairs(prior), op=ADD)
+            first = GCOLS if i < GP_TILES else 0
+            if first < D:
+                nc.vector.tensor_tensor(out=y[i][:, first:], in0=y_scaled[i][:, first:], in1=prior[:, first:], op=ADD)
 
         def round_y(i):
             if i < VCAST:
@@ -270,82 +295,65 @@ def tile_collection_concept_scores_k7_kernel(
                     out=out_2[0, 4 * quadrant:4 * quadrant + 4, first * P:last * P].bitcast(I32),
                     in_=y_plane[32 * quadrant:32 * quadrant + 4, first * P:last * P].bitcast(I32))
 
-        for step in range(TILES):
-            if step >= 3:
-                turn_z(step - 3)
-            if step % TILES_PER_COLLECTION == 2:
-                spread_term(step // TILES_PER_COLLECTION, 0)
-            if step % TILES_PER_COLLECTION == 0 and step >= 4:
-                spread_term(step // TILES_PER_COLLECTION - 1, 1)
-            if step % 2 == 1:
-                spread_factor(step // TILES_PER_COLLECTION, step % TILES_PER_COLLECTION // 2)
-            if S_SORT and step + 1 < TILES:
-                sort_words(nc.scalar.copy, step + 1, PASSES - S_SORT, S_SORT)
-            turn_queries(step)
-            group_queries(step)
-            if step >= 5:
+        def live(i):
+            return 0 <= i < TILES
+
+        def turn_small(step):
+            small = psum.tile([P, 2, 2, P], F32, name="small", tag="z_bank")
+            staging = small[:, 1].rearrange("r j p -> r (j p)")
+            if live(step - 3):
+                turn(z_bf[step - 3], None, small[:, 0])
+            if live(step - 1):
+                spread_row(*divmod(step - 1, TILES_PER_COLLECTION), staging)
+            if live(step - 3):
+                z_grouped[step - 3] = group(small[:, 0], "z_grouped")
+            if live(step - 1):
+                keep_row(*divmod(step - 1, TILES_PER_COLLECTION), staging)
+
+        for step in range(TILES + 5):
+            if live(step - 3):
+                turn_small(step)
+            if step == TILES and EARLY:
+                first_product(step - 1)
+            if live(step):
+                turn_queries(step)
+                group_queries(step)
+            if step in (1, 2):
+                turn_small(step)
+            if step == 0:
+                turn_rows()
+            if live(step - 5) and (step <= TILES or not YLATE):
                 turn_y(step - 5)
-            if step >= 2:
+            if live(step - 2):
                 scale_z(step - 2)
-            if step >= 4:
-                scale_y(step - 4)
-            if step >= 2:
-                shift_z(step - 2)
-            if step >= 3:
+            if live(step - 3):
                 quantise_z(step - 3)
-            if step >= 4:
-                shift_y(step - 4)
-            if V_SORT and step + 1 < TILES:
-                sort_words(nc.vector.tensor_copy, step + 1, PASSES - n_sorted, V_SORT)
-            quantise_queries(step)
-            if step >= 5:
+            if step > TILES and YLATE:
+                if live(step - 3):
+                    second_product(step - 3)
+                turn_y(step - 5)
+            if live(step - 4):
+                scale_y(step - 4)
+            if live(step - 2):
+                shift_z(step - 2)
+            if live(step - 5) and step > TILES and QFIRST:
                 quantise_y(step - 5)
                 store_codes(step - 5)
-            if step >= 4:
+            if live(step - 4):
+                shift_y(step - 4)
+            if live(step):
+                quantise_queries(step)
+            if live(step - 5) and not (step > TILES and QFIRST):
+                quantise_y(step - 5)
+                store_codes(step - 5)
+            if step - 5 == TILES - TILES_PER_COLLECTION - 1:
+                store_plane(0, TILES - TILES_PER_COLLECTION)
+            if live(step - 4):
                 round_y(step - 4)
-            if step >= 1:
+            if S_SORT and SORT_FROM <= step + 1 < TILES:
+                sort_words(nc.scalar.copy, step + 1, PASSES - S_SORT, S_SORT)
+            if live(step - 1) and not (step == TILES and EARLY):
                 first_product(step - 1)
-            if step >= 3:
+            if live(step - 3) and not (step > TILES and YLATE):
                 second_product(step - 3)
-
-        spread_term(G - 1, 1)
-        turn_z(13)
-        first_product(15)
-        turn_y(11)
-        scale_z(14)
-        scale_y(12)
-        shift_z(14)
-        quantise_z(13)
-        scale_z(15)
-        shift_y(12)
-        shift_z(15)
-        turn_z(14)
-        second_product(13)
-        round_y(12)
-        quantise_y(11)
-        store_codes(11)
-        store_plane(0, 12)
-        turn_z(15)
-        quantise_z(14)
-        scale_y(13)
-        second_product(14)
-        turn_y(12)
-        quantise_z(15)
-        second_product(15)
-        shift_y(13)
-        scale_y(14)
-        round_y(13)
-        scale_y(15)
-        shift_y(14)
-        quantise_y(12)
-        turn_y(13)
-        round_y(14)
-        shift_y(15)
-        turn_y(14)
-        turn_y(15)
-        round_y(15)
-        quantise_y(13)
-        quantise_y(14)
-        quantise_y(15)
-        store_codes(15)
-        store_plane(12, 16)
+        store_plane(TILES - TILES_PER_COLLECTION, TILES)

@@ -18,21 +18,24 @@ ADD = mybir.AluOpType.add
 
 P = 128
 PASSES = T // 512
+PAIRS = 256
 TILES_PER_COLLECTION = R // P
 TILES = G * TILES_PER_COLLECTION
-GP_TILES = 12
-V_SORT = 0
-G_SORT = 0
-S_SORT = 1
-SORT_FROM = 2
-EARLY = 1
-YLATE = 0
-QFIRST = 0
-GCOLS = 256
-LAG = 0
-Z_FIRST = TILES
-QSPLIT = 15
-VCAST = 15
+LAST = TILES - 1
+SCALE, SHIFT, GAIN, PRIOR = range(4)
+
+POOL_COLUMNS = D // 2
+POOL_COLLECTIONS = G - 1
+SORTED_PASSES = PASSES // 2
+FIRST_SORTED_TILE = 2
+
+
+def sorted_pairs(ap):
+    return ap.rearrange("r (p u e) -> r u p e", u=2, e=2)
+
+
+def as_sorted(ap):
+    return ap.rearrange("r (u p e) -> r u p e", u=2, e=2)
 
 
 def tile_collection_concept_scores_k7_kernel(
@@ -60,8 +63,8 @@ def tile_collection_concept_scores_k7_kernel(
         doc = keep.tile([P, G, 2 * D], U8, name="doc", align_bytes=64)
         doc_plane = keep.tile([P, G * D], U8, name="doc_plane", align_bytes=64)
         row_raw = keep.tile([P, P], F32, name="row_raw", align_bytes=64)
-        row_words = keep.tile([P, 8 * G], F32, name="row_words", align_bytes=64)
-        terms = psum.tile([P, 2, 2 * P], F32, name="terms")
+        row_columns = keep.tile([P, 8 * G], F32, name="row_columns", align_bytes=64)
+        terms = psum.tile([P, 2, PAIRS], F32, name="terms")
         y = [keep.tile([P, D], F32, name="y%d" % i, align_bytes=64) for i in range(TILES)]
         y_codes = [keep.tile([P, R], U32, name="y_codes%d" % a, align_bytes=64) for a in range(G)]
         y_plane = keep.tile([P, G * R], U8, name="y_plane", align_bytes=64)
@@ -75,99 +78,121 @@ def tile_collection_concept_scores_k7_kernel(
             for n, piece in enumerate(q_raw[i]):
                 nc.sync.dma_start(out=piece[:], in_=query_rows[i * P:(i + 1) * P, n * width:(n + 1) * width])
 
-        def pass_words(i, first, count):
-            width = T // len(q_raw[i]) // 512
-            piece = q_raw[i][first // width]
-            return piece[:].bitcast(F32)[:, 256 * (first % width):256 * (first % width + count)]
-
-        def load_words(tile, words):
-            nc.sync.dma_start(out=tile[:].bitcast(I32), in_=words.rearrange("g p n -> p g n").bitcast(I32))
-
-        def load_plane(plane, scales):
-            groups = scales.shape[0]
+        def load_weight(words_tile, plane, words, scales):
+            nc.sync.dma_start(out=words_tile[:].bitcast(I32), in_=words.rearrange("g p n -> p g n").bitcast(I32))
             for quadrant in range(4):
-                rows = plane[32 * quadrant:32 * quadrant + 4, :].rearrange("r (g n) -> r g n", g=groups)
+                live = plane[32 * quadrant:32 * quadrant + 4, :].rearrange("r (g n) -> r g n", g=scales.shape[0])
                 nc.sync.dma_start(
-                    out=rows.bitcast(I32),
+                    out=live.bitcast(I32),
                     in_=scales[:, 4 * quadrant:4 * quadrant + 4, :].rearrange("g r n -> r g n").bitcast(I32),
                 )
 
         def load_term(a):
-            load_words(term[a], term_words[PASSES * a:PASSES * (a + 1)])
-            load_plane(term_plane[a], term_scales[PASSES * a:PASSES * (a + 1)])
-
-        def load_row(n, vector):
-            nc.sync.dma_start(
-                out=row_raw[2 * G * n:2 * G * (n + 1), :],
-                in_=vector.rearrange("a (j m) -> (a j) m", j=2).bitcast(F32))
+            groups = slice(PASSES * a, PASSES * (a + 1))
+            load_weight(term[a], term_plane[a], term_words[groups], term_scales[groups])
 
         load_queries(0)
         for n, vector in enumerate((concept_scale, concept_shift, doc_gain, doc_prior)):
-            load_row(n, vector)
+            nc.sync.dma_start(
+                out=row_raw[2 * G * n:2 * G * (n + 1), :],
+                in_=vector.rearrange("a (j m) -> (a j) m", j=2).bitcast(F32))
         load_queries(1)
         load_term(0)
         load_queries(2)
         load_queries(3)
-        load_words(doc, doc_words)
-        load_plane(doc_plane, doc_scales)
+        load_weight(doc, doc_plane, doc_words, doc_scales)
         load_queries(4)
         for i in range(5, TILES):
-            if i % TILES_PER_COLLECTION == 1 and i < TILES - 1:
+            if i % TILES_PER_COLLECTION == 1:
                 load_term(i // TILES_PER_COLLECTION)
             load_queries(i)
 
-        n_sorted = V_SORT + S_SORT + G_SORT
-        q_sorted, q_banks, q_bf, q_codes, q_plane, h, z_scaled, z_bf, z_bank, z_grouped = (
-            {}, {}, {}, {}, {}, {}, {}, {}, {}, {})
-        z_codes, z_plane, score, y_scaled, y_bf, y_bank, y_grouped = {}, {}, {}, {}, {}, {}, {}
+        q_sorted, q_banks, q_grouped, q_codes, q_plane, h = {}, {}, {}, {}, {}, {}
+        z_scaled, z_bf, z_grouped, z_codes, z_plane, score = {}, {}, {}, {}, {}, {}
+        y_scaled, y_bf, y_grouped, rows = {}, {}, {}, {}
 
-        def sorted_pairs(ap):
-            return ap.rearrange("r (p u e) -> r u p e", u=2, e=2)
+        def collection(i):
+            return i // TILES_PER_COLLECTION
 
-        rows = {}
+        def query_pairs(i, first, count):
+            per_piece = PASSES // len(q_raw[i])
+            at = first % per_piece
+            return q_raw[i][first // per_piece][:].bitcast(F32)[:, PAIRS * at:PAIRS * (at + count)]
 
-        def sort_words(copy, i, first, count):
-            if i not in q_sorted:
-                q_sorted[i] = work.tile([P, n_sorted, 2, P], F32, name="q_sorted", align_bytes=64, bufs=1 if G_SORT else 3)
-            at = first - (PASSES - n_sorted)
-            copy(out=q_sorted[i][:, at:at + count],
-                 in_=pass_words(i, first, count).rearrange("r (g p u) -> r g u p", u=2, g=count))
+        def spare_bank(name):
+            return psum.tile([P, C], F32, name=name, tag="q_bank", bufs=3)
+
+
+        def turn_rows():
+            bank = psum.tile([P, P], F32, name="bank", tag="y_bank")
+            nc.tensor.transpose(bank[:], row_raw[:], identity[:])
+            nc.scalar.copy(out=row_columns[:], in_=bank[:, :8 * G])
+
+        def spread_row(a, n, staging):
+            for j in range(2):
+                staged = n in (SCALE, GAIN) or (n == PRIOR and a < POOL_COLLECTIONS and j == 0)
+                out = staging if staged else terms[:, n // 2]
+                column = 2 * G * n + 2 * a + j
+                nc.tensor.transpose(
+                    out[:, j * P:(j + 1) * P], row_columns[:, column:column + 1].to_broadcast([P, P]), identity[:])
+
+        def keep_row(a, n, staging):
+            if n == SCALE:
+                rows[n, a] = work.tile([P, PAIRS], F32, name="scale", bufs=2)
+                nc.scalar.copy(out=rows[n, a][:].rearrange("r (u p) -> r u p", u=2),
+                               in_=staging.rearrange("r (p u) -> r u p", u=2))
+            elif n == GAIN:
+                rows[n, a] = work.tile([P, PAIRS], F32, name="gain", bufs=2)
+                nc.scalar.copy(out=rows[n, a][:], in_=staging)
+            elif n == PRIOR:
+                rows[n, a] = work.tile([P, P], F32, name="prior", bufs=2)
+                nc.scalar.copy(out=rows[n, a][:], in_=staging[:, :P])
+
+
+        def sort_queries(i):
+            q_sorted[i] = work.tile([P, SORTED_PASSES, 2, P], F32, name="q_sorted", align_bytes=64)
+            nc.scalar.copy(
+                out=q_sorted[i][:],
+                in_=query_pairs(i, PASSES - SORTED_PASSES, SORTED_PASSES).rearrange(
+                    "r (g p u) -> r g u p", u=2, g=SORTED_PASSES))
 
         def turn_queries(i):
             q_banks[i] = []
-            q_banks[i] = [None, None]
-            for half in ((1, 0) if G_SORT else (0, 1)):
+            for half in range(2):
                 bank = psum.tile([P, 2, 2, P], F32, name="q_bank", tag="q_bank", bufs=3)
                 for g in range(2 * half, 2 * half + 2):
                     for u in range(2):
-                        if i in q_sorted and g >= PASSES - n_sorted:
-                            words = q_sorted[i][:, g - (PASSES - n_sorted), u, :]
+                        if i in q_sorted and g >= PASSES - SORTED_PASSES:
+                            pairs = q_sorted[i][:, g - (PASSES - SORTED_PASSES), u, :]
                         else:
-                            words = pass_words(i, g, 1)[:, u::2]
-                        nc.tensor.transpose(bank[:, g % 2, u, :], words, identity[:])
-                q_banks[i][half] = bank
+                            pairs = query_pairs(i, g, 1)[:, u::2]
+                        nc.tensor.transpose(bank[:, g % 2, u, :], pairs, identity[:])
+                q_banks[i].append(bank)
 
         def group_queries(i):
-            q_bf[i] = [work.tile([P, 2 * P * 4], BF16, name="q_bf%d" % half, align_bytes=64) for half in range(2)] \
-                if i >= QSPLIT else [work.tile([P, PASSES * P * 4], BF16, name="q_bf", align_bytes=64)]
-            for half in ((1, 0) if G_SORT else (0, 1)):
-                out = q_bf[i][half][:] if i >= QSPLIT else q_bf[i][0][:, half * 1024:(half + 1) * 1024]
+            if i == LAST:
+                q_grouped[i] = [work.tile([P, T // 2], BF16, name="q_grouped%d" % half, align_bytes=64)
+                                for half in range(2)]
+                halves = [piece[:] for piece in q_grouped[i]]
+            else:
+                q_grouped[i] = [work.tile([P, T], BF16, name="q_grouped", align_bytes=64)]
+                halves = [q_grouped[i][0][:, :T // 2], q_grouped[i][0][:, T // 2:]]
+            for out, bank in zip(halves, q_banks[i]):
                 nc.scalar.copy(
                     out=out.bitcast(F32).rearrange("p (g r u) -> p g r u", u=2, g=2),
-                    in_=q_banks[i][half][:].rearrange("p g u r -> p g r u"))
+                    in_=bank[:].rearrange("p g u r -> p g r u"))
 
         def quantise_queries(i):
             q_codes[i] = work.tile([P, PASSES * P], U32, name="q_codes", align_bytes=64)
             q_plane[i] = work.tile([P, PASSES * P], U8, name="q_plane", align_bytes=64)
-            width = PASSES * P // len(q_bf[i])
-            for n, piece in enumerate(q_bf[i]):
+            width = PASSES * P // len(q_grouped[i])
+            for n, piece in enumerate(q_grouped[i]):
                 part = slice(n * width, (n + 1) * width)
                 nc.vector.quantize_mx(out=q_codes[i][:, part].bitcast(FP8X4), scales=q_plane[i][:, part], in_=piece[:])
 
         def first_product(i):
-            a = i // TILES_PER_COLLECTION
-            h[i] = (psum.tile([P, C], F32, name="h", tag="h") if i < TILES - 1
-                    else psum.tile([P, C], F32, name="last_h", tag="q_bank", bufs=3))
+            a = collection(i)
+            h[i] = spare_bank("last_h") if i == LAST else psum.tile([P, C], F32, name="h", tag="h")
             for g in range(PASSES):
                 nc.tensor.matmul_mx(
                     out=h[i][:],
@@ -177,61 +202,46 @@ def tile_collection_concept_scores_k7_kernel(
                     rhs_scale=term_plane[a][:, g * C:(g + 1) * C],
                     start=(g == 0), stop=(g == PASSES - 1))
 
-        def turn_rows():
-            bank = psum.tile([P, P], F32, name="bank", tag="y_bank")
-            nc.tensor.transpose(bank[:], row_raw[:], identity[:])
-            nc.scalar.copy(out=row_words[:], in_=bank[:, :8 * G])
-
-        def spread(n, a, j, out):
-            column = 2 * G * n + 2 * a + j
-            nc.tensor.transpose(
-                out[:, j * P:(j + 1) * P], row_words[:, column:column + 1].to_broadcast([P, P]), identity[:])
-
-        def spread_row(a, n, staging):
-            shared = n == 3 and a * TILES_PER_COLLECTION < GP_TILES
-            for j in range(2):
-                spread(n, a, j, staging if n % 2 == 0 or (shared and j == 0) else terms[:, n // 2])
-
-        def keep_row(a, n, staging):
-            if n == 0:
-                rows[n, a] = work.tile([P, 2 * P], F32, name="scale", bufs=2)
-                nc.scalar.copy(out=rows[n, a][:].rearrange("r (u p) -> r u p", u=2),
-                               in_=staging.rearrange("r (p u) -> r u p", u=2))
-            elif n == 2:
-                rows[n, a] = work.tile([P, 2 * P], F32, name="gain", bufs=2)
-                nc.scalar.copy(out=rows[n, a][:], in_=staging)
-            elif n == 3 and a * TILES_PER_COLLECTION < GP_TILES:
-                rows[n, a] = work.tile([P, P], F32, name="prior", bufs=2)
-                nc.scalar.copy(out=rows[n, a][:], in_=staging[:, :P])
 
         def scale_z(i):
             z_scaled[i] = work.tile([P, C], F32, name="z_scaled")
             nc.vector.tensor_tensor(
-                out=z_scaled[i][:].rearrange("r (u p e) -> r u p e", u=2, e=2), in0=sorted_pairs(h[i][:]),
-                in1=rows[0, i // TILES_PER_COLLECTION][:].bitcast(BF16).rearrange("r (u p e) -> r u p e", u=2, e=2),
-                op=MULT)
+                out=as_sorted(z_scaled[i][:]), in0=sorted_pairs(h[i][:]),
+                in1=as_sorted(rows[SCALE, collection(i)][:].bitcast(BF16)), op=MULT)
 
         def shift_z(i):
             z_bf[i] = work.tile([P, C], BF16, name="z_bf", align_bytes=64)
             nc.vector.tensor_tensor(
-                out=z_bf[i][:].rearrange("r (u p e) -> r u p e", u=2, e=2),
-                in0=z_scaled[i][:].rearrange("r (u p e) -> r u p e", u=2, e=2),
+                out=as_sorted(z_bf[i][:]), in0=as_sorted(z_scaled[i][:]),
                 in1=sorted_pairs(terms[:, 0].bitcast(BF16)), op=ADD)
 
-        def turn(source, name, bank=None):
-            if bank is None:
-                bank = psum.tile([P, 2, P], F32, name="bank", tag=name)
-            words = source[:].bitcast(F32)
+        def turn(source, bank):
+            pairs = source[:].bitcast(F32)
             for u in range(2):
-                nc.tensor.transpose(bank[:, u, :], words[:, u * P:(u + 1) * P], identity[:])
-            return bank
+                nc.tensor.transpose(bank[:, u, :], pairs[:, u * P:(u + 1) * P], identity[:])
 
         def group(bank, name):
             grouped = work.tile([P, P * 4], BF16, name=name, align_bytes=64)
             nc.scalar.copy(
                 out=grouped[:].bitcast(F32).rearrange("p (r u) -> p r u", u=2),
-                in_=bank[:].rearrange("p u r -> p r u"))
+                in_=bank.rearrange("p u r -> p r u"))
             return grouped
+
+        def turn_z(i):
+            bank = psum.tile([P, 2, P], F32, name="bank", tag="z_bank")
+            turn(z_bf[i], bank)
+            z_grouped[i] = group(bank[:], "z_grouped")
+
+        def turn_z_and_spread(step):
+            bank = psum.tile([P, 2, 2, P], F32, name="bank", tag="z_bank")
+            staging = bank[:, 1].rearrange("r j p -> r (j p)")
+            a, n = divmod(step - 1, TILES_PER_COLLECTION)
+            if step >= 3:
+                turn(z_bf[step - 3], bank[:, 0])
+            spread_row(a, n, staging)
+            if step >= 3:
+                z_grouped[step - 3] = group(bank[:, 0], "z_grouped")
+            keep_row(a, n, staging)
 
         def quantise_z(i):
             z_codes[i] = work.tile([P, P], U32, name="z_codes", align_bytes=64)
@@ -239,38 +249,46 @@ def tile_collection_concept_scores_k7_kernel(
             nc.vector.quantize_mx(out=z_codes[i][:].bitcast(FP8X4), scales=z_plane[i][:], in_=z_grouped[i][:])
 
         def second_product(i):
-            a = i // TILES_PER_COLLECTION
-            score[i] = (psum.tile([P, D], F32, name="score") if i < TILES - 2
-                        else psum.tile([P, D], F32, name="late_score", tag="q_bank", bufs=3))
+            a = collection(i)
+            score[i] = spare_bank("late_score") if i >= LAST - 1 else psum.tile([P, D], F32, name="score")
             nc.tensor.matmul_mx(
                 out=score[i][:],
                 lhsT=z_codes[i][:].bitcast(FP8X4), lhsT_scale=z_plane[i][:],
                 rhs=doc[:, a, :].bitcast(FP4X4), rhs_scale=doc_plane[:, a * D:(a + 1) * D],
                 start=True, stop=True)
 
+
         def scale_y(i):
+            a = collection(i)
             y_scaled[i] = work.tile([P, D], F32, name="y_scaled", bufs=4)
-            nc.vector.tensor_tensor(out=y_scaled[i][:], in0=score[i][:], in1=rows[2, i // TILES_PER_COLLECTION][:].bitcast(BF16), op=MULT)
-            if i < GP_TILES:
+            nc.vector.tensor_tensor(out=y_scaled[i][:], in0=score[i][:], in1=rows[GAIN, a][:].bitcast(BF16), op=MULT)
+            if a < POOL_COLLECTIONS:
                 nc.gpsimd.tensor_tensor(
-                    out=y[i][:, :GCOLS], in0=y_scaled[i][:, :GCOLS], in1=rows[3, i // TILES_PER_COLLECTION][:].bitcast(BF16), op=ADD)
+                    out=y[i][:, :POOL_COLUMNS], in0=y_scaled[i][:, :POOL_COLUMNS],
+                    in1=rows[PRIOR, a][:].bitcast(BF16), op=ADD)
 
         def shift_y(i):
+            first = POOL_COLUMNS if collection(i) < POOL_COLLECTIONS else 0
             prior = terms[:, 1].bitcast(BF16)
-            if i >= VCAST:
-                y_bf[i] = work.tile([P, D], BF16, name="y_bf", align_bytes=64)
-                nc.vector.tensor_tensor(
-                    out=y_bf[i][:].rearrange("r (u p e) -> r u p e", u=2, e=2),
-                    in0=sorted_pairs(y_scaled[i][:]), in1=sorted_pairs(prior), op=ADD)
-            first = GCOLS if i < GP_TILES else 0
-            if first < D:
-                nc.vector.tensor_tensor(out=y[i][:, first:], in0=y_scaled[i][:, first:], in1=prior[:, first:], op=ADD)
+            nc.vector.tensor_tensor(out=y[i][:, first:], in0=y_scaled[i][:, first:], in1=prior[:, first:], op=ADD)
 
         def round_y(i):
-            if i < VCAST:
-                y_bf[i] = work.tile([P, D], BF16, name="y_bf", align_bytes=64)
-                nc.scalar.copy(out=y_bf[i][:].rearrange("r (u p e) -> r u p e", u=2, e=2), in_=sorted_pairs(y[i][:]))
+            y_bf[i] = work.tile([P, D], BF16, name="y_bf", align_bytes=64)
+            nc.scalar.copy(out=as_sorted(y_bf[i][:]), in_=sorted_pairs(y[i][:]))
+
+        def shift_and_round_y(i):
+            y_bf[i] = work.tile([P, D], BF16, name="y_bf", align_bytes=64)
+            nc.vector.tensor_tensor(
+                out=as_sorted(y_bf[i][:]), in0=sorted_pairs(y_scaled[i][:]),
+                in1=sorted_pairs(terms[:, 1].bitcast(BF16)), op=ADD)
+
+        def store_y(i):
             nc.sync.dma_start(out=y_rows[i * P:(i + 1) * P, :], in_=y[i][:])
+
+        def turn_y(i, tag="y_bank"):
+            bank = psum.tile([P, 2, P], F32, name="bank", tag=tag)
+            turn(y_bf[i], bank)
+            y_grouped[i] = group(bank[:], "y_grouped")
 
         def quantise_y(i):
             a, j = divmod(i, TILES_PER_COLLECTION)
@@ -278,82 +296,96 @@ def tile_collection_concept_scores_k7_kernel(
                 out=y_codes[a][:, j * P:(j + 1) * P].bitcast(FP8X4),
                 scales=y_plane[:, i * P:(i + 1) * P], in_=y_grouped[i][:])
 
-        def store_codes(i):
-            a, j = divmod(i, TILES_PER_COLLECTION)
-            if j == TILES_PER_COLLECTION - 1:
-                nc.sync.dma_start(out=y_words[:, a * R:(a + 1) * R], in_=y_codes[a][:].bitcast(I32))
+        def store_codes(a):
+            nc.sync.dma_start(out=y_words[:, a * R:(a + 1) * R], in_=y_codes[a][:].bitcast(I32))
 
-        def turn_z(i):
-            z_grouped[i] = group(turn(z_bf[i], "z_bank"), "z_grouped")
-
-        def turn_y(i):
-            y_grouped[i] = group(turn(y_bf[i], {TILES - 2: "h", TILES - 1: "z_bank"}.get(i, "y_bank")), "y_grouped")
-
-        def store_plane(first, last):
+        def store_scales(first, last):
             for quadrant in range(4):
                 nc.sync.dma_start(
-                    out=out_2[0, 4 * quadrant:4 * quadrant + 4, first * P:last * P].bitcast(I32),
-                    in_=y_plane[32 * quadrant:32 * quadrant + 4, first * P:last * P].bitcast(I32))
+                    out=out_2[0, 4 * quadrant:4 * quadrant + 4, first * R:last * R].bitcast(I32),
+                    in_=y_plane[32 * quadrant:32 * quadrant + 4, first * R:last * R].bitcast(I32))
 
-        def live(i):
-            return 0 <= i < TILES
-
-        def turn_small(step):
-            small = psum.tile([P, 2, 2, P], F32, name="small", tag="z_bank")
-            staging = small[:, 1].rearrange("r j p -> r (j p)")
-            if live(step - 3):
-                turn(z_bf[step - 3], None, small[:, 0])
-            if live(step - 1):
-                spread_row(*divmod(step - 1, TILES_PER_COLLECTION), staging)
-            if live(step - 3):
-                z_grouped[step - 3] = group(small[:, 0], "z_grouped")
-            if live(step - 1):
-                keep_row(*divmod(step - 1, TILES_PER_COLLECTION), staging)
-
-        for step in range(TILES + 5):
-            if live(step - 3):
-                turn_small(step)
-            if step == TILES and EARLY:
-                first_product(step - 1)
-            if live(step):
-                turn_queries(step)
-                group_queries(step)
-            if step in (1, 2):
-                turn_small(step)
+        for step in range(TILES):
+            if step >= 3:
+                turn_z_and_spread(step)
+            turn_queries(step)
+            group_queries(step)
             if step == 0:
                 turn_rows()
-            if live(step - 5) and (step <= TILES or not YLATE):
+            elif step < 3:
+                turn_z_and_spread(step)
+            if step >= 5:
                 turn_y(step - 5)
-            if live(step - 2):
+            if step >= 2:
                 scale_z(step - 2)
-            if live(step - 3):
-                quantise_z(step - 3)
-            if step > TILES and YLATE:
-                if live(step - 3):
-                    second_product(step - 3)
-                turn_y(step - 5)
-            if live(step - 4):
+            if step >= 4:
                 scale_y(step - 4)
-            if live(step - 2):
+            if step >= 3:
+                quantise_z(step - 3)
+            if step >= 2:
                 shift_z(step - 2)
-            if live(step - 5) and step > TILES and QFIRST:
-                quantise_y(step - 5)
-                store_codes(step - 5)
-            if live(step - 4):
+            if step >= 4:
                 shift_y(step - 4)
-            if live(step):
-                quantise_queries(step)
-            if live(step - 5) and not (step > TILES and QFIRST):
+            quantise_queries(step)
+            if step >= 5:
                 quantise_y(step - 5)
-                store_codes(step - 5)
-            if step - 5 == TILES - TILES_PER_COLLECTION - 1:
-                store_plane(0, TILES - TILES_PER_COLLECTION)
-            if live(step - 4):
+                if (step - 5) % TILES_PER_COLLECTION == TILES_PER_COLLECTION - 1:
+                    store_codes(collection(step - 5))
+            if FIRST_SORTED_TILE <= step + 1 < TILES:
+                sort_queries(step + 1)
+            if step >= 4:
                 round_y(step - 4)
-            if S_SORT and SORT_FROM <= step + 1 < TILES:
-                sort_words(nc.scalar.copy, step + 1, PASSES - S_SORT, S_SORT)
-            if live(step - 1) and not (step == TILES and EARLY):
+                store_y(step - 4)
+            if step >= 1:
                 first_product(step - 1)
-            if live(step - 3) and not (step > TILES and YLATE):
+            if step >= 3:
                 second_product(step - 3)
-        store_plane(TILES - TILES_PER_COLLECTION, TILES)
+
+        t0, t1, t2, t3 = range(TILES - TILES_PER_COLLECTION, TILES)
+        spread_row(G - 1, PRIOR, None)
+        turn_z(t1)
+        first_product(t3)
+        turn_y(t0 - 1)
+
+        scale_z(t2)
+        scale_y(t0)
+        shift_z(t2)
+        quantise_z(t1)
+        scale_z(t3)
+        shift_y(t0)
+        shift_z(t3)
+        turn_z(t2)
+        second_product(t1)
+        round_y(t0)
+        store_y(t0)
+        quantise_y(t0 - 1)
+        store_codes(G - 2)
+        store_scales(0, G - 1)
+
+        turn_z(t3)
+        quantise_z(t2)
+        scale_y(t1)
+        second_product(t2)
+        turn_y(t0)
+        quantise_z(t3)
+        second_product(t3)
+        shift_y(t1)
+        scale_y(t2)
+        round_y(t1)
+        store_y(t1)
+
+        scale_y(t3)
+        shift_y(t2)
+        quantise_y(t0)
+        turn_y(t1)
+        round_y(t2)
+        store_y(t2)
+        shift_and_round_y(t3)
+        shift_y(t3)
+        turn_y(t2, "h")
+        turn_y(t3, "z_bank")
+        store_y(t3)
+        for i in (t1, t2, t3):
+            quantise_y(i)
+        store_codes(G - 1)
+        store_scales(G - 1, G)

from contextlib import ExitStack

import concourse.mybir as mybir
from concourse.masks import make_identity

G, R, T, C, D = 4, 512, 2048, 512, 512
FLOPS = 2 * G * R * (T * C + C * D)

F32 = mybir.dt.float32
BF16 = mybir.dt.bfloat16
I32 = mybir.dt.int32
U32 = mybir.dt.uint32
U8 = mybir.dt.uint8
FP8X4 = mybir.dt.float8_e4m3fn_x4
FP4X4 = mybir.dt.float4_e2m1fn_x4
MULT = mybir.AluOpType.mult
ADD = mybir.AluOpType.add

P = 128
PASSES = T // 512
PAIRS = 256
TILES_PER_COLLECTION = R // P
TILES = G * TILES_PER_COLLECTION
LAST = TILES - 1
SCALE, SHIFT, GAIN, PRIOR = range(4)

POOL_COLUMNS = D // 2
POOL_COLLECTIONS = G - 1
SORTED_PASSES = PASSES // 2
FIRST_SORTED_TILE = 2


def sorted_pairs(ap):
    return ap.rearrange("r (p u e) -> r u p e", u=2, e=2)


def as_sorted(ap):
    return ap.rearrange("r (u p e) -> r u p e", u=2, e=2)


def tile_collection_concept_scores_k7_kernel(
    tc, queries, term_words, term_scales, concept_scale, concept_shift,
    doc_words, doc_scales, doc_gain, doc_prior, out_0, out_1, out_2,
):
    nc = tc.nc
    query_rows = queries.rearrange("a r k -> (a r) k")
    y_rows = out_0.rearrange("a r d -> (a r) d")
    y_words = out_1[0].rearrange("p m t -> p (m t)").bitcast(I32)

    with ExitStack() as ctx:
        keep = ctx.enter_context(tc.tile_pool(name="keep", bufs=1))
        work = ctx.enter_context(tc.tile_pool(name="work", bufs=3))
        psum = ctx.enter_context(tc.psum_pool(name="psum", bufs=1))
        ctx.enter_context(tc.manual_schedule())

        identity = keep.tile([P, P], F32, name="identity")
        make_identity(nc, identity[:])

        q_raw = [[keep.tile([P, T // 2], BF16, name="q_raw%d_%d" % (i, half), align_bytes=64) for half in range(2)]
                 if i == 0 else [keep.tile([P, T], BF16, name="q_raw%d" % i, align_bytes=64)] for i in range(TILES)]
        term = [keep.tile([P, PASSES, 2 * C], U8, name="term%d" % a, align_bytes=64) for a in range(G)]
        term_plane = [keep.tile([P, PASSES * C], U8, name="term_plane%d" % a, align_bytes=64) for a in range(G)]
        doc = keep.tile([P, G, 2 * D], U8, name="doc", align_bytes=64)
        doc_plane = keep.tile([P, G * D], U8, name="doc_plane", align_bytes=64)
        row_raw = keep.tile([P, P], F32, name="row_raw", align_bytes=64)
        row_columns = keep.tile([P, 8 * G], F32, name="row_columns", align_bytes=64)
        terms = psum.tile([P, 2, PAIRS], F32, name="terms")
        y = [keep.tile([P, D], F32, name="y%d" % i, align_bytes=64) for i in range(TILES)]
        y_codes = [keep.tile([P, R], U32, name="y_codes%d" % a, align_bytes=64) for a in range(G)]
        y_plane = keep.tile([P, G * R], U8, name="y_plane", align_bytes=64)

        nc.vector.memset(row_raw[:], 0.0)
        for plane in term_plane + [doc_plane]:
            nc.vector.memset(plane[:].bitcast(I32), 0)

        def load_queries(i):
            width = T // len(q_raw[i])
            for n, piece in enumerate(q_raw[i]):
                nc.sync.dma_start(out=piece[:], in_=query_rows[i * P:(i + 1) * P, n * width:(n + 1) * width])

        def load_weight(words_tile, plane, words, scales):
            nc.sync.dma_start(out=words_tile[:].bitcast(I32), in_=words.rearrange("g p n -> p g n").bitcast(I32))
            for quadrant in range(4):
                live = plane[32 * quadrant:32 * quadrant + 4, :].rearrange("r (g n) -> r g n", g=scales.shape[0])
                nc.sync.dma_start(
                    out=live.bitcast(I32),
                    in_=scales[:, 4 * quadrant:4 * quadrant + 4, :].rearrange("g r n -> r g n").bitcast(I32),
                )

        def load_term(a):
            groups = slice(PASSES * a, PASSES * (a + 1))
            load_weight(term[a], term_plane[a], term_words[groups], term_scales[groups])

        load_queries(0)
        for n, vector in enumerate((concept_scale, concept_shift, doc_gain, doc_prior)):
            nc.sync.dma_start(
                out=row_raw[2 * G * n:2 * G * (n + 1), :],
                in_=vector.rearrange("a (j m) -> (a j) m", j=2).bitcast(F32))
        load_queries(1)
        load_term(0)
        load_queries(2)
        load_queries(3)
        load_weight(doc, doc_plane, doc_words, doc_scales)
        load_queries(4)
        for i in range(5, TILES):
            if i % TILES_PER_COLLECTION == 1:
                load_term(i // TILES_PER_COLLECTION)
            load_queries(i)

        q_sorted, q_banks, q_grouped, q_codes, q_plane, h = {}, {}, {}, {}, {}, {}
        z_scaled, z_bf, z_grouped, z_codes, z_plane, score = {}, {}, {}, {}, {}, {}
        y_scaled, y_bf, y_grouped, rows = {}, {}, {}, {}

        def collection(i):
            return i // TILES_PER_COLLECTION

        def query_pairs(i, first, count):
            per_piece = PASSES // len(q_raw[i])
            at = first % per_piece
            return q_raw[i][first // per_piece][:].bitcast(F32)[:, PAIRS * at:PAIRS * (at + count)]

        def spare_bank(name):
            return psum.tile([P, C], F32, name=name, tag="q_bank", bufs=3)


        def turn_rows():
            bank = psum.tile([P, P], F32, name="bank", tag="y_bank")
            nc.tensor.transpose(bank[:], row_raw[:], identity[:])
            nc.scalar.copy(out=row_columns[:], in_=bank[:, :8 * G])

        def spread_row(a, n, staging):
            for j in range(2):
                staged = n in (SCALE, GAIN) or (n == PRIOR and a < POOL_COLLECTIONS and j == 0)
                out = staging if staged else terms[:, n // 2]
                column = 2 * G * n + 2 * a + j
                nc.tensor.transpose(
                    out[:, j * P:(j + 1) * P], row_columns[:, column:column + 1].to_broadcast([P, P]), identity[:])

        def keep_row(a, n, staging):
            if n == SCALE:
                rows[n, a] = work.tile([P, PAIRS], F32, name="scale", bufs=2)
                nc.scalar.copy(out=rows[n, a][:].rearrange("r (u p) -> r u p", u=2),
                               in_=staging.rearrange("r (p u) -> r u p", u=2))
            elif n == GAIN:
                rows[n, a] = work.tile([P, PAIRS], F32, name="gain", bufs=2)
                nc.scalar.copy(out=rows[n, a][:], in_=staging)
            elif n == PRIOR:
                rows[n, a] = work.tile([P, P], F32, name="prior", bufs=2)
                nc.scalar.copy(out=rows[n, a][:], in_=staging[:, :P])


        def sort_queries(i):
            q_sorted[i] = work.tile([P, SORTED_PASSES, 2, P], F32, name="q_sorted", align_bytes=64)
            nc.scalar.copy(
                out=q_sorted[i][:],
                in_=query_pairs(i, PASSES - SORTED_PASSES, SORTED_PASSES).rearrange(
                    "r (g p u) -> r g u p", u=2, g=SORTED_PASSES))

        def turn_queries(i):
            q_banks[i] = []
            for half in range(2):
                bank = psum.tile([P, 2, 2, P], F32, name="q_bank", tag="q_bank", bufs=3)
                for g in range(2 * half, 2 * half + 2):
                    for u in range(2):
                        if i in q_sorted and g >= PASSES - SORTED_PASSES:
                            pairs = q_sorted[i][:, g - (PASSES - SORTED_PASSES), u, :]
                        else:
                            pairs = query_pairs(i, g, 1)[:, u::2]
                        nc.tensor.transpose(bank[:, g % 2, u, :], pairs, identity[:])
                q_banks[i].append(bank)

        def group_queries(i):
            if i == LAST:
                q_grouped[i] = [work.tile([P, T // 2], BF16, name="q_grouped%d" % half, align_bytes=64)
                                for half in range(2)]
                halves = [piece[:] for piece in q_grouped[i]]
            else:
                q_grouped[i] = [work.tile([P, T], BF16, name="q_grouped", align_bytes=64)]
                halves = [q_grouped[i][0][:, :T // 2], q_grouped[i][0][:, T // 2:]]
            for out, bank in zip(halves, q_banks[i]):
                nc.scalar.copy(
                    out=out.bitcast(F32).rearrange("p (g r u) -> p g r u", u=2, g=2),
                    in_=bank[:].rearrange("p g u r -> p g r u"))

        def quantise_queries(i):
            q_codes[i] = work.tile([P, PASSES * P], U32, name="q_codes", align_bytes=64)
            q_plane[i] = work.tile([P, PASSES * P], U8, name="q_plane", align_bytes=64)
            width = PASSES * P // len(q_grouped[i])
            for n, piece in enumerate(q_grouped[i]):
                part = slice(n * width, (n + 1) * width)
                nc.vector.quantize_mx(out=q_codes[i][:, part].bitcast(FP8X4), scales=q_plane[i][:, part], in_=piece[:])

        def first_product(i):
            a = collection(i)
            h[i] = spare_bank("last_h") if i == LAST else psum.tile([P, C], F32, name="h", tag="h")
            for g in range(PASSES):
                nc.tensor.matmul_mx(
                    out=h[i][:],
                    lhsT=q_codes[i][:, g * P:(g + 1) * P].bitcast(FP8X4),
                    lhsT_scale=q_plane[i][:, g * P:(g + 1) * P],
                    rhs=term[a][:, g, :].bitcast(FP4X4),
                    rhs_scale=term_plane[a][:, g * C:(g + 1) * C],
                    start=(g == 0), stop=(g == PASSES - 1))


        def scale_z(i):
            z_scaled[i] = work.tile([P, C], F32, name="z_scaled")
            nc.vector.tensor_tensor(
                out=as_sorted(z_scaled[i][:]), in0=sorted_pairs(h[i][:]),
                in1=as_sorted(rows[SCALE, collection(i)][:].bitcast(BF16)), op=MULT)

        def shift_z(i):
            z_bf[i] = work.tile([P, C], BF16, name="z_bf", align_bytes=64)
            nc.vector.tensor_tensor(
                out=as_sorted(z_bf[i][:]), in0=as_sorted(z_scaled[i][:]),
                in1=sorted_pairs(terms[:, 0].bitcast(BF16)), op=ADD)

        def turn(source, bank):
            pairs = source[:].bitcast(F32)
            for u in range(2):
                nc.tensor.transpose(bank[:, u, :], pairs[:, u * P:(u + 1) * P], identity[:])

        def group(bank, name):
            grouped = work.tile([P, P * 4], BF16, name=name, align_bytes=64)
            nc.scalar.copy(
                out=grouped[:].bitcast(F32).rearrange("p (r u) -> p r u", u=2),
                in_=bank.rearrange("p u r -> p r u"))
            return grouped

        def turn_z(i):
            bank = psum.tile([P, 2, P], F32, name="bank", tag="z_bank")
            turn(z_bf[i], bank)
            z_grouped[i] = group(bank[:], "z_grouped")

        def turn_z_and_spread(step):
            bank = psum.tile([P, 2, 2, P], F32, name="bank", tag="z_bank")
            staging = bank[:, 1].rearrange("r j p -> r (j p)")
            a, n = divmod(step - 1, TILES_PER_COLLECTION)
            if step >= 3:
                turn(z_bf[step - 3], bank[:, 0])
            spread_row(a, n, staging)
            if step >= 3:
                z_grouped[step - 3] = group(bank[:, 0], "z_grouped")
            keep_row(a, n, staging)

        def quantise_z(i):
            z_codes[i] = work.tile([P, P], U32, name="z_codes", align_bytes=64)
            z_plane[i] = work.tile([P, P], U8, name="z_plane", align_bytes=64)
            nc.vector.quantize_mx(out=z_codes[i][:].bitcast(FP8X4), scales=z_plane[i][:], in_=z_grouped[i][:])

        def second_product(i):
            a = collection(i)
            score[i] = spare_bank("late_score") if i >= LAST - 1 else psum.tile([P, D], F32, name="score")
            nc.tensor.matmul_mx(
                out=score[i][:],
                lhsT=z_codes[i][:].bitcast(FP8X4), lhsT_scale=z_plane[i][:],
                rhs=doc[:, a, :].bitcast(FP4X4), rhs_scale=doc_plane[:, a * D:(a + 1) * D],
                start=True, stop=True)


        def scale_y(i):
            a = collection(i)
            y_scaled[i] = work.tile([P, D], F32, name="y_scaled", bufs=4)
            nc.vector.tensor_tensor(out=y_scaled[i][:], in0=score[i][:], in1=rows[GAIN, a][:].bitcast(BF16), op=MULT)
            if a < POOL_COLLECTIONS:
                nc.gpsimd.tensor_tensor(
                    out=y[i][:, :POOL_COLUMNS], in0=y_scaled[i][:, :POOL_COLUMNS],
                    in1=rows[PRIOR, a][:].bitcast(BF16), op=ADD)

        def shift_y(i):
            first = POOL_COLUMNS if collection(i) < POOL_COLLECTIONS else 0
            prior = terms[:, 1].bitcast(BF16)
            nc.vector.tensor_tensor(out=y[i][:, first:], in0=y_scaled[i][:, first:], in1=prior[:, first:], op=ADD)

        def round_y(i):
            y_bf[i] = work.tile([P, D], BF16, name="y_bf", align_bytes=64)
            nc.scalar.copy(out=as_sorted(y_bf[i][:]), in_=sorted_pairs(y[i][:]))

        def shift_and_round_y(i):
            y_bf[i] = work.tile([P, D], BF16, name="y_bf", align_bytes=64)
            nc.vector.tensor_tensor(
                out=as_sorted(y_bf[i][:]), in0=sorted_pairs(y_scaled[i][:]),
                in1=sorted_pairs(terms[:, 1].bitcast(BF16)), op=ADD)

        def store_y(i):
            nc.sync.dma_start(out=y_rows[i * P:(i + 1) * P, :], in_=y[i][:])

        def turn_y(i, tag="y_bank"):
            bank = psum.tile([P, 2, P], F32, name="bank", tag=tag)
            turn(y_bf[i], bank)
            y_grouped[i] = group(bank[:], "y_grouped")

        def quantise_y(i):
            a, j = divmod(i, TILES_PER_COLLECTION)
            nc.vector.quantize_mx(
                out=y_codes[a][:, j * P:(j + 1) * P].bitcast(FP8X4),
                scales=y_plane[:, i * P:(i + 1) * P], in_=y_grouped[i][:])

        def store_codes(a):
            nc.sync.dma_start(out=y_words[:, a * R:(a + 1) * R], in_=y_codes[a][:].bitcast(I32))

        def store_scales(first, last):
            for quadrant in range(4):
                nc.sync.dma_start(
                    out=out_2[0, 4 * quadrant:4 * quadrant + 4, first * R:last * R].bitcast(I32),
                    in_=y_plane[32 * quadrant:32 * quadrant + 4, first * R:last * R].bitcast(I32))

        for step in range(TILES):
            if step >= 3:
                turn_z_and_spread(step)
            turn_queries(step)
            group_queries(step)
            if step == 0:
                turn_rows()
            elif step < 3:
                turn_z_and_spread(step)
            if step >= 5:
                turn_y(step - 5)
            if step >= 2:
                scale_z(step - 2)
            if step >= 4:
                scale_y(step - 4)
            if step >= 3:
                quantise_z(step - 3)
            if step >= 2:
                shift_z(step - 2)
            if step >= 4:
                shift_y(step - 4)
            quantise_queries(step)
            if step >= 5:
                quantise_y(step - 5)
                if (step - 5) % TILES_PER_COLLECTION == TILES_PER_COLLECTION - 1:
                    store_codes(collection(step - 5))
            if FIRST_SORTED_TILE <= step + 1 < TILES:
                sort_queries(step + 1)
            if step >= 4:
                round_y(step - 4)
                store_y(step - 4)
            if step >= 1:
                first_product(step - 1)
            if step >= 3:
                second_product(step - 3)

        t0, t1, t2, t3 = range(TILES - TILES_PER_COLLECTION, TILES)
        spread_row(G - 1, PRIOR, None)
        turn_z(t1)
        first_product(t3)
        turn_y(t0 - 1)

        scale_z(t2)
        scale_y(t0)
        shift_z(t2)
        quantise_z(t1)
        scale_z(t3)
        shift_y(t0)
        shift_z(t3)
        turn_z(t2)
        second_product(t1)
        round_y(t0)
        store_y(t0)
        quantise_y(t0 - 1)
        store_codes(G - 2)
        store_scales(0, G - 1)

        turn_z(t3)
        quantise_z(t2)
        scale_y(t1)
        second_product(t2)
        turn_y(t0)
        quantise_z(t3)
        second_product(t3)
        shift_y(t1)
        scale_y(t2)
        round_y(t1)
        store_y(t1)

        scale_y(t3)
        shift_y(t2)
        quantise_y(t0)
        turn_y(t1)
        round_y(t2)
        store_y(t2)
        shift_and_round_y(t3)
        shift_y(t3)
        turn_y(t2, "h")
        turn_y(t3, "z_bank")
        store_y(t3)
        for i in (t1, t2, t3):
            quantise_y(i)
        store_codes(G - 1)
        store_scales(G - 1, G)
